import numpy as np
import ml_dtypes


def mxq(x, axis, fmt="e4m3"):
    dtype, down = {"e4m3": (ml_dtypes.float8_e4m3fn, 7), "e5m2": (ml_dtypes.float8_e5m2, 14)}[fmt]
    v = np.moveaxis(np.asarray(x, np.float32).astype(ml_dtypes.bfloat16).astype(np.float64), axis, -1)
    blocks = v.reshape(v.shape[:-1] + (-1, 32))
    amax = np.abs(blocks).max(-1, keepdims=True)
    byte = np.maximum(np.where(amax > 0, np.frexp(amax)[1] - 1 + 127, 0) - down, 1)
    scale = np.exp2(byte - 127.0)
    codes = (blocks / scale).astype(np.float32).astype(dtype).astype(np.float64)
    return np.moveaxis((codes * scale).reshape(v.shape), -1, axis)


WIDE = False


def mx_kscale(k):
    if not WIDE:
        return np.ones(k)
    levels = np.array([10, -10, 5, -5, 0])
    if k % 512:
        return np.exp2(np.random.permutation(np.resize(levels, k // 32))).repeat(32)
    a = np.empty((k // 512, 16))
    for p in range(k // 512):
        a[p, :8] = np.random.permutation(np.resize(levels, 8))
        for g in range(8):
            far = levels[np.abs(levels - a[p, g]) >= 10]
            a[p, g + 8] = far[np.random.randint(len(far))]
    return np.exp2(a.ravel()).repeat(32)


BF16 = ml_dtypes.bfloat16


def bf(x):
    return np.asarray(x, np.float32).astype(BF16)


def f64(x):
    return np.asarray(x).astype(np.float64)


E2M1 = np.array([0.0, 0.5, 1.0, 1.5, 2.0, 3.0, 4.0, 6.0, -0.0, -0.5, -1.0, -1.5, -2.0, -3.0, -4.0, -6.0])


def pack_weight(w, fmt):
    k, n = w.shape
    w = f64(bf(w)).reshape(k // 32, 32, n)
    amax = np.abs(w).max(1)
    if fmt == "e4m3":
        byte = np.frexp(amax)[1] - 1 + 127 - 7
    else:
        mant, ex = np.frexp(amax / 6.0)
        byte = np.where(mant > 0.5, ex, ex - 1) + 127
    byte = np.clip(np.where(amax > 0, byte, 1), 1, 254)
    scaled = (w * np.exp2(127.0 - byte)[:, None, :]).reshape(k, n).astype(np.float32)
    by_word = np.ascontiguousarray(scaled.reshape(k // 512, 128, 4, n).transpose(0, 1, 3, 2))
    if fmt == "e4m3":
        words = by_word.astype(ml_dtypes.float8_e4m3fn).view(np.uint8)
    else:
        c = by_word.astype(ml_dtypes.float4_e2m1fn).view(np.uint8) & 0xF
        words = c[..., 0::2] | (c[..., 1::2] << 4)
    return np.ascontiguousarray(words), np.ascontiguousarray(byte.astype(np.uint8).reshape(k // 512, 16, n))


def unpack_weight(words, scales, fmt):
    g, p, n, _ = words.shape
    if fmt == "e4m3":
        vals = np.ascontiguousarray(words).view(ml_dtypes.float8_e4m3fn).astype(np.float64)
    else:
        nib = np.empty((g, p, n, 4), np.uint8)
        nib[..., 0::2] = words & 0xF
        nib[..., 1::2] = words >> 4
        vals = E2M1[nib]
    vals = vals * np.repeat(np.exp2(scales.astype(np.float64) - 127.0), 8, axis=1)[..., None]
    return vals.transpose(0, 1, 3, 2).reshape(g * 512, n)
def pack4(w):
    words, scales = pack_weight(w, "e2m1")
    return words.reshape(words.shape[0], 128, -1), scales


def unpack4(words, scales):
    return unpack_weight(words.reshape(words.shape[0], 128, -1, 2), scales, "e2m1")


M, K, N, R, P = 2048, 1024, 1024, 512, 512


def setup_inputs():
    s, c, u = mx_kscale(K), mx_kscale(N), mx_kscale(M)
    x = np.random.standard_normal((M, K)) * s
    beta = 0.7 * np.random.standard_normal((K, N)) / np.sqrt(K) / s[:, None]
    num = (0.25 + 0.75 * np.random.random_sample((M, N))) * c * u[:, None]
    z = np.random.standard_normal((M, P)) / np.sqrt(M) / u[:, None]
    v = np.random.standard_normal((N, R)) / np.sqrt(N) / c[:, None]
    v_words, v_scales = pack4(v)
    return {"x": bf(x), "beta": bf(beta), "num": bf(num), "z": bf(z),
            "v_words": v_words, "v_scales": v_scales}


def reference(x, beta, num, z, v_words, v_scales):
    eta = mxq(f64(x), 1, "e4m3") @ mxq(f64(beta), 0, "e4m3")
    sw = f64(num) * (1.0 + np.exp(eta))
    contrast = mxq(sw, 1, "e4m3") @ unpack4(v_words, v_scales)
    moment = mxq(f64(z), 0, "e4m3").T @ mxq(sw, 0, "e4m3")
    return contrast, moment

@@ -1,0 +1,378 @@
+from contextlib import ExitStack
+
+import concourse.mybir as mybir
+from concourse.masks import make_identity
+
+M, K, N, R, PZ = 2048, 1024, 1024, 512, 512
+FLOPS = 2 * M * K * N + 2 * M * N * R + 2 * PZ * M * N
+
+F32 = mybir.dt.float32
+BF16 = mybir.dt.bfloat16
+U32 = mybir.dt.uint32
+I32 = mybir.dt.int32
+U8 = mybir.dt.uint8
+FP8X4 = mybir.dt.float8_e4m3fn_x4
+FP4X4 = mybir.dt.float4_e2m1fn_x4
+ALU = mybir.AluOpType
+ACT = mybir.ActivationFunctionType
+
+P = 128
+W = 512
+STEPS = 16
+ORDER = [(0, 0), (0, 1), (1, 0), (2, 0), (3, 0), (1, 1), (2, 1), (3, 1)]
+X_IT = [-2,-1,1,2,3,4,6,7]
+CON_IT = [5,8,13,14,16,16,17,19]
+MOM_IT = [9,11,12,13,15,15,18,18]
+MOM_OUT_V = [0, 1]
+B_IT = [0,0,0,0]
+Z_IT = [4,5,6,7,8,9,10,11]
+Z_V = [128,128,128,128,0,0,0,0]
+LOADS = "x1 b2 b3 n0 x2 n1 x3 n2 x4 z0 x5 n3 v z1 x6 x7 n4 z2 z3"
+SWT_LAG = 1
+TPAIR = 99
+CON_V = 16
+IL_IT = [2,3,4,5,6,7,8,9,10,11,12,13,14,15,16,16]
+CON_E = [0,0,0,0,0,0,0,0]
+T_IT = [1,2,3,4,5,6,7,8,9,10,11,12,13,14,15,16]
+T_E = [0,0,0,0,0,0,0,0,0,0,0,0,0,0,0,0]
+B_V = [256,0,256,0]
+MO_E = [1,0,1,1,0,1,0,1]
+PE_ORD = [0,0,0,0,0,0,0,0,0,0,0,0,0,0,0,0,0,0,0,0]
+NE = 2
+NC = 2
+NG = 4
+
+
+def tile_inverse_propensity_weighted_sums_s8_kernel(tc, x, beta, num, z, v_words, v_scales, out_0, out_1):
+    nc = tc.nc
+    with ExitStack() as ctx:
+        sb = ctx.enter_context(tc.tile_pool(name="sb", bufs=1))
+        ps = ctx.enter_context(tc.psum_pool(name="ps", bufs=1))
+        ctx.enter_context(tc.manual_schedule())
+
+        def tiles(name, count, shape, dtype):
+            return [sb.tile(shape, dtype, name="%s%d" % (name, i), align_bytes=64) for i in range(count)]
+
+        bank = [ps.tile([P, W], F32, name="bank%d" % i) for i in range(8)]
+        held = {}
+        ring = [0]
+
+        def take(key, it):
+            size = 8 if it < MOM_IT[0] else 4
+            held[key] = bank[ring[0] % size]
+            ring[0] = (ring[0] + 1) % size
+            return held[key]
+
+
+        ident = sb.tile([P, P], F32, name="ident", align_bytes=64)
+        warm = sb.tile([P, 8], F32, name="warm", align_bytes=64)
+        x_first = tiles("x_first", 2, [P, K], BF16)
+        x_raw = tiles("x_raw", 7, [P, 2, K], BF16)
+        beta_raw = tiles("beta_raw", 4, [P, 4, W], BF16)
+        z_raw = tiles("z_raw", 4, [P, 4, W], BF16)
+        num_raw = tiles("num_raw", 5, [P, 4, W], BF16)
+        v_codes = sb.tile([P, 2, 2 * W], U8, name="v_codes", align_bytes=64)
+        v_plane = sb.tile([P, 2, W], U8, name="v_plane", align_bytes=64)
+
+        x_codes, x_plane = tiles("x_codes", 8, [P, W], U32), tiles("x_plane", 8, [P, W], U8)
+        beta_codes, beta_plane = tiles("beta_codes", 4, [P, W], U32), tiles("beta_plane", 4, [P, W], U8)
+        z_codes, z_plane = tiles("z_codes", 4, [P, W], U32), tiles("z_plane", 4, [P, W], U8)
+        swm_codes, swm_plane = tiles("swm_codes", 8, [P, W], U32), tiles("swm_plane", 8, [P, W], U8)
+        swn_codes, swn_plane = tiles("swn_codes", 16, [P, 2 * P], U32), tiles("swn_plane", 16, [P, 2 * P], U8)
+
+        xt = tiles("xt", 2, [P, 2, 2 * W], BF16)
+        grouped = tiles("grouped", NG, [P, W // 2, 4], BF16)
+        swm = tiles("swm", 4, [P, W // 2, 4], BF16)
+        expo = tiles("expo", NE, [P, 2, 2, 2 * P], F32)
+        sw = tiles("sw", NC, [P, 2, 4, 2 * P], BF16)
+        swn = tiles("swn", 2, [P, 2 * W], BF16)
+        con_out = tiles("con_out", 3, [P, 2, W], F32)
+        mom_out = tiles("mom_out", 4, [P, W], F32)
+
+        x_v = x.rearrange("(j p t) k -> j p t k", p=P, t=4)
+        num_v = num.rearrange("(j p t) n -> j p t n", p=P, t=4)
+        z_v = z.rearrange("(j p t) c -> j p t c", p=P, t=4)
+        beta_v = beta.rearrange("(c p t) n -> c p t n", p=P, t=4)
+        out0_v = out_0.rearrange("(j p t) r -> j p t r", p=P, t=4)
+
+        def x_rows(i, tt):
+            if i == 0:
+                return x_first[tt][:]
+            return x_raw[(i - 1) % len(x_raw)][:, tt, :]
+
+        def load_x(i):
+            nc.sync.dma_start(out=x_raw[(i - 1) % len(x_raw)][:], in_=x_v[i // 2][:, 2 * (i % 2) : 2 * (i % 2) + 2, :])
+
+        def load_beta(g, c):
+            nc.sync.dma_start(out=beta_raw[2 * g + c][:], in_=beta_v[c][:, :, g * W : (g + 1) * W])
+
+        def load_num(u):
+            j, g = ORDER[u]
+            nc.sync.dma_start(out=num_raw[u % 5][:], in_=num_v[j][:, :, g * W : (g + 1) * W])
+
+        def load_z(j):
+            nc.sync.dma_start(out=z_raw[j][:], in_=z_v[j])
+
+        def load_v():
+            nc.sync.dma_start(out=v_codes[:].bitcast(I32), in_=v_words.rearrange("g p b -> p g b").bitcast(I32))
+            for q in range(4):
+                nc.sync.dma_start(
+                    out=v_plane[32 * q : 32 * q + 4, :, :].bitcast(I32),
+                    in_=v_scales[:, 4 * q : 4 * q + 4, :].rearrange("g r n -> r g n").bitcast(I32),
+                )
+
+        def interleave(copy, dst, src, half, c0, c1):
+            lo = half * W // 2
+            copy(
+                out=dst[:, c0:c1, :].rearrange("p (c i) t -> p c t i", i=4),
+                in_=src[:, :, lo + c0 : lo + c1].rearrange("p t (c i) -> p c t i", i=4),
+            )
+
+        def quantize_half(codes, plane, half, values):
+            cols = slice(half * W // 2, (half + 1) * W // 2)
+            quantize(codes[:, cols], plane[:, cols], flat(values[:]))
+
+        def quantize(codes, plane, values):
+            nc.vector.quantize_mx(out=codes.bitcast(FP8X4), scales=plane, in_=values)
+
+        def flat(t3):
+            return t3.rearrange("p a b -> p (a b)")
+
+        def x_transpose(i, it):
+            for tt in range(2):
+                acc = take(("x", i, tt), it)
+                words = x_rows(i, tt).bitcast(F32)
+                for c in range(2):
+                    for u in range(2):
+                        col = (2 * c + u) * P
+                        nc.tensor.transpose(
+                            acc[:, col : col + P], words[:, 256 * c + u : 256 * (c + 1) : 2], ident[:]
+                        )
+
+        def x_evict(i, tt):
+            nc.scalar.copy(
+                out=xt[i % 2][:, tt, :].bitcast(F32).rearrange("p (c m u) -> p c m u", c=2, u=2),
+                in_=held["x", i, tt][:].rearrange("p (c u m) -> p c m u", c=2, u=2),
+            )
+
+        def x_quantize(i):
+            quantize(x_codes[i][:], x_plane[i][:], flat(xt[i % 2][:]))
+
+        def eta(s, tt):
+            j, g = ORDER[s // 2]
+            i = 2 * j + s % 2
+            acc = take(("e", s, tt), s)
+            for c in range(2):
+                cols = slice((2 * tt + c) * P, (2 * tt + c + 1) * P)
+                nc.tensor.matmul_mx(
+                    out=acc[:],
+                    lhsT=x_codes[i][:, cols].bitcast(FP8X4),
+                    lhsT_scale=x_plane[i][:, cols],
+                    rhs=beta_codes[2 * g + c][:].bitcast(FP8X4),
+                    rhs_scale=beta_plane[2 * g + c][:],
+                    start=(c == 0),
+                    stop=(c == 1),
+                )
+
+        def exp(s, tt):
+            nc.scalar.activation(
+                out=expo[s % NE][:, :, tt, :].rearrange("p u (q e) -> p u q e", e=2),
+                in_=held["e", s, tt][:].rearrange("p (q u e) -> p u q e", u=2, e=2),
+                func=ACT.Exp,
+            )
+
+        def weigh(s):
+            unit, h = divmod(s, 2)
+            pairs = flat(num_raw[unit % 5][:, 2 * h : 2 * h + 2, :]).rearrange("p (a u e) -> p u a e", u=2, e=2)
+            for u in range(2):
+                nc.vector.scalar_tensor_tensor(
+                    out=flat(sw[unit % NC][:, u, 2 * h : 2 * h + 2, :]).rearrange("p (a e) -> p a e", e=2),
+                    in0=flat(expo[s % NE][:, u, :, :]).rearrange("p (a e) -> p a e", e=2),
+                    scalar=1.0,
+                    in1=pairs[:, u, :, :],
+                    op0=ALU.add,
+                    op1=ALU.mult,
+                )
+
+        def sw_transpose(s, it):
+            acc = take(("t", s), it)
+            unit, h = divmod(s, 2)
+            for tt in range(2):
+                for u in range(2):
+                    col = (2 * tt + u) * P
+                    nc.tensor.transpose(
+                        acc[:, col : col + P], sw[unit % NC][:, u, 2 * h + tt, :].bitcast(F32), ident[:]
+                    )
+
+        def sw_evict(s):
+            (nc.vector.tensor_copy if T_E[s] else nc.scalar.copy)(
+                out=swn[s % 2][:].bitcast(F32).rearrange("p (t m u) -> p t m u", t=2, u=2),
+                in_=held["t", s][:].rearrange("p (t u m) -> p t m u", t=2, u=2),
+            )
+
+        def swn_quantize(s):
+            j, g = ORDER[s // 2]
+            i = 8 * g + 2 * j + s % 2
+            quantize(swn_codes[i][:], swn_plane[i][:], swn[s % 2][:])
+
+        def swm_interleave(unit, u):
+            nc.vector.tensor_copy(
+                out=swm[(2 * unit + u) % 4][:].rearrange("p (c i) t -> p c t i", i=4),
+                in_=sw[unit % NC][:, u, :, :].rearrange("p t (c i) -> p c t i", i=4),
+            )
+
+        def swm_quantize(unit, u):
+            j, g = ORDER[unit]
+            quantize_half(swm_codes[4 * g + j], swm_plane[4 * g + j], u, swm[(2 * unit + u) % 4])
+
+        def contrast(i, tt, it):
+            acc = take(("c", i, tt), it)
+            for g in range(2):
+                cols = slice(tt * P, (tt + 1) * P)
+                nc.tensor.matmul_mx(
+                    out=acc[:],
+                    lhsT=swn_codes[8 * g + i][:, cols].bitcast(FP8X4),
+                    lhsT_scale=swn_plane[8 * g + i][:, cols],
+                    rhs=v_codes[:, g, :].bitcast(FP4X4),
+                    rhs_scale=v_plane[:, g, :],
+                    start=(g == 0),
+                    stop=(g == 1),
+                )
+
+        def contrast_evict(copy, i, tt):
+            copy(out=con_out[i % 3][:, tt, :], in_=held["c", i, tt][:])
+
+        def contrast_store(i):
+            j, h = divmod(i, 2)
+            nc.sync.dma_start(out=out0_v[j][:, 2 * h : 2 * h + 2, :], in_=con_out[i % 3][:])
+
+        def moment(g, b, acc, groups):
+            cols = slice(b * P, (b + 1) * P)
+            for j in groups:
+                nc.tensor.matmul_mx(
+                    out=acc[:],
+                    lhsT=z_codes[j][:, cols].bitcast(FP8X4),
+                    lhsT_scale=z_plane[j][:, cols],
+                    rhs=swm_codes[4 * g + j][:].bitcast(FP8X4),
+                    rhs_scale=swm_plane[4 * g + j][:],
+                    start=(j == 0),
+                    stop=(j == 3),
+                )
+
+        def moment_out(copy, g, b, acc):
+            copy(
+                out=mom_out[b][:].rearrange("p (q u e) -> p q u e", u=2, e=2),
+                in_=acc[:].rearrange("p (u q e) -> p q u e", u=2, e=2),
+            )
+            nc.sync.dma_start(out=out_1[b * P : (b + 1) * P, g * W : (g + 1) * W], in_=mom_out[b][:])
+
+        load_beta(0, 0)
+        nc.sync.dma_start(out=x_first[0][:], in_=x_v[0][:, 0, :])
+        load_beta(0, 1)
+        nc.sync.dma_start(out=x_first[1][:], in_=x_v[0][:, 1, :])
+        make_identity(nc, ident[:])
+        nc.vector.memset(warm[:], 0.0)
+        nc.scalar.activation(out=warm[:, 4:5], in_=warm[:, 0:1], func=ACT.Exp)
+        nc.vector.memset(flat(v_plane[:]).bitcast(I32), 0)
+        for name in LOADS.split():
+            k = int(name[1:] or "0")
+            if name[0] == "x":
+                load_x(k)
+            elif name[0] == "b":
+                load_beta(k // 2, k % 2)
+            elif name[0] == "z":
+                load_z(k)
+            elif name[0] == "v":
+                load_v()
+            elif k < 5:
+                load_num(k)
+        HW = W // 2
+
+        x_transpose(0, -2)
+        interleave(nc.vector.tensor_copy, grouped[0], beta_raw[0], 0, 0, HW)
+        interleave(nc.scalar.copy, grouped[1], beta_raw[0], 1, 0, HW)
+        x_evict(0, 0)
+        quantize_half(beta_codes[0], beta_plane[0], 0, grouped[0])
+        interleave(nc.vector.tensor_copy, grouped[2], beta_raw[1], 0, 0, HW)
+        quantize_half(beta_codes[0], beta_plane[0], 1, grouped[1])
+        interleave(nc.vector.tensor_copy, grouped[3], beta_raw[1], 1, 0, HW)
+        x_evict(0, 1)
+        quantize_half(beta_codes[1], beta_plane[1], 0, grouped[2])
+        x_transpose(1, -1)
+        x_quantize(0)
+        quantize_half(beta_codes[1], beta_plane[1], 1, grouped[3])
+        x_evict(1, 0)
+        x_evict(1, 1)
+
+        il_it = {}
+        for k in range(16):
+            il_it[k // 2, k % 2] = IL_IT[k]
+        t_it = T_IT
+        for it in range(STEPS + 4):
+            if 0 <= it - 1 < STEPS:
+                weigh(it - 1)
+                if (it - 1) % 2 == 1 and 5 <= (it - 1) // 2 + 5 < 8:
+                    load_num((it - 1) // 2 + 5)
+            for k in range(4):
+                if B_IT[k] + 1 == it:
+                    quantize_half(beta_codes[2 + k // 2], beta_plane[2 + k // 2], k % 2, grouped[k % NG])
+            for k in range(8):
+                if Z_IT[k] + 1 == it:
+                    quantize_half(z_codes[k // 2], z_plane[k // 2], k % 2, grouped[k % NG])
+            for i in range(1, 8):
+                if X_IT[i] + 1 == it:
+                    x_quantize(i)
+            for key in il_it:
+                if il_it[key] + 1 == it:
+                    swm_quantize(*key)
+            for s in range(STEPS):
+                if t_it[s] + 1 == it:
+                    swn_quantize(s)
+            for key in il_it:
+                if il_it[key] == it:
+                    swm_interleave(*key)
+            for k in range(4):
+                if B_IT[k] == it and B_V[k] > 0:
+                    interleave(nc.vector.tensor_copy, grouped[k % NG], beta_raw[2 + k // 2], k % 2, 0, B_V[k])
+            for k in range(8):
+                if Z_IT[k] == it and Z_V[k] > 0:
+                    interleave(nc.vector.tensor_copy, grouped[k % NG], z_raw[k // 2], k % 2, 0, Z_V[k])
+            if it < STEPS:
+                eta(it, 0)
+                eta(it, 1)
+                exp(it, 0)
+                exp(it, 1)
+            for part in ["mct", "cmt", "tcm", "tmc", "ctm", "mtc"][PE_ORD[it]]:
+                if part == "m":
+                    for k in range(8):
+                        if MOM_IT[k] == it:
+                            for b in range(4):
+                                moment(k // 4, b, bank[4 + b], range(k % 4, k % 4 + 1))
+                if part == "c":
+                    for i in range(8):
+                        if CON_IT[i] == it:
+                            contrast(i, 0, it)
+                            contrast_evict(nc.scalar.copy, i, 0)
+                            contrast(i, 1, it)
+                            contrast_evict(nc.scalar.copy if CON_E[i] == 0 else nc.vector.tensor_copy, i, 1)
+                            contrast_store(i)
+                if part == "t":
+                    for s in range(STEPS):
+                        if t_it[s] == it:
+                            sw_transpose(s, it)
+                            sw_evict(s)
+                    for i in range(2, 8):
+                        if X_IT[i] == it:
+                            x_transpose(i, it)
+                            x_evict(i, 0)
+                            x_evict(i, 1)
+            for k in range(4):
+                if B_IT[k] == it and B_V[k] < HW:
+                    interleave(nc.scalar.copy, grouped[k % NG], beta_raw[2 + k // 2], k % 2, B_V[k], HW)
+            for k in range(8):
+                if Z_IT[k] == it and Z_V[k] < HW:
+                    interleave(nc.scalar.copy, grouped[k % NG], z_raw[k // 2], k % 2, Z_V[k], HW)
+            for g in range(2):
+                if MOM_IT[4 * g + 3] == it:
+                    for b in range(4):
+                        moment_out(nc.vector.tensor_copy if MO_E[4 * g + b] else nc.scalar.copy, g, b, bank[4 + b])

@@ -19,27 +19,31 @@ ACT = mybir.ActivationFunctionType
 P = 128
 W = 512
 STEPS = 16
-ORDER = [(0, 0), (0, 1), (1, 0), (2, 0), (3, 0), (1, 1), (2, 1), (3, 1)]
-X_IT = [-2,-1,1,2,3,4,6,7]
-CON_IT = [5,8,13,14,16,16,17,19]
-MOM_IT = [9,11,12,13,15,15,18,18]
+ORDER = [(0, 0), (1, 0), (0, 1), (2, 0), (3, 0), (1, 1), (2, 1), (3, 1)]
+X_IT = [-2,-1,0,1,3,4,5,6]
+CON_IT = [8,9,14,15,16,17,17,19]
+MOM_IT = [9,10,11,13,14,15,17,18]
 MOM_OUT_V = [0, 1]
-B_IT = [0,0,0,0]
+B_IT = [1,1,2,2]
 Z_IT = [4,5,6,7,8,9,10,11]
-Z_V = [128,128,128,128,0,0,0,0]
-LOADS = "x1 b2 b3 n0 x2 n1 x3 n2 x4 z0 x5 n3 v z1 x6 x7 n4 z2 z3"
+Z_V = [128,128,128,128,64,64,64,64]
+LOADS = "x1 n0 x2 b2 x3 n1 b3 x4 n2 z0 x5 v n3 z1 x6 x7 n4 z2 z3 n5 n6 n7"
 SWT_LAG = 1
 TPAIR = 99
 CON_V = 16
 IL_IT = [2,3,4,5,6,7,8,9,10,11,12,13,14,15,16,16]
-CON_E = [0,0,0,0,0,0,0,0]
-T_IT = [1,2,3,4,5,6,7,8,9,10,11,12,13,14,15,16]
+CON_E = [0,0,0,0,0,0,0,1]
+T_IT = [2,3,4,5,6,7,8,9,10,11,12,13,14,15,15,16]
+S_IT = [1,2,3,4,5,6,7,8,9,10,11,12,13,14,15,16]
+V_ORD = [0,0,0,0,0,0,0,0,0,0,0,0,0,0,0,0,0,0,0,0]
+X_E = [0,0,0,0,0,0,0,0]
+NX = 5
 T_E = [0,0,0,0,0,0,0,0,0,0,0,0,0,0,0,0]
-B_V = [256,0,256,0]
-MO_E = [1,0,1,1,0,1,0,1]
-PE_ORD = [0,0,0,0,0,0,0,0,0,0,0,0,0,0,0,0,0,0,0,0]
-NE = 2
-NC = 2
+B_V = [192,192,192,192]
+MO_E = [1,0,1,0,0,1,0,1]
+PE_ORD = [4,4,4,4,4,4,4,4,4,4,4,4,4,4,4,4,4,4,4,4]
+HEAD = [320,320]
+NC = 3
 NG = 4
 
 
@@ -67,9 +71,9 @@ def tile_inverse_propensity_weighted_sums_s8_kernel(tc, x, beta, num, z, v_words
         ident = sb.tile([P, P], F32, name="ident", align_bytes=64)
         warm = sb.tile([P, 8], F32, name="warm", align_bytes=64)
         x_first = tiles("x_first", 2, [P, K], BF16)
-        x_raw = tiles("x_raw", 7, [P, 2, K], BF16)
+        x_raw = tiles("x_raw", NX, [P, 2, K], BF16)
         beta_raw = tiles("beta_raw", 4, [P, 4, W], BF16)
-        z_raw = tiles("z_raw", 4, [P, 4, W], BF16)
+        z_raw = tiles("z_raw", 2, [P, 4, W], BF16) + beta_raw[:2]
         num_raw = tiles("num_raw", 5, [P, 4, W], BF16)
         v_codes = sb.tile([P, 2, 2 * W], U8, name="v_codes", align_bytes=64)
         v_plane = sb.tile([P, 2, W], U8, name="v_plane", align_bytes=64)
@@ -78,14 +82,14 @@ def tile_inverse_propensity_weighted_sums_s8_kernel(tc, x, beta, num, z, v_words
         beta_codes, beta_plane = tiles("beta_codes", 4, [P, W], U32), tiles("beta_plane", 4, [P, W], U8)
         z_codes, z_plane = tiles("z_codes", 4, [P, W], U32), tiles("z_plane", 4, [P, W], U8)
         swm_codes, swm_plane = tiles("swm_codes", 8, [P, W], U32), tiles("swm_plane", 8, [P, W], U8)
-        swn_codes, swn_plane = tiles("swn_codes", 16, [P, 2 * P], U32), tiles("swn_plane", 16, [P, 2 * P], U8)
+        swn_codes, swn_plane = tiles("swn_codes", 8, [P, W], U32), tiles("swn_plane", 8, [P, W], U8)
 
         xt = tiles("xt", 2, [P, 2, 2 * W], BF16)
-        grouped = tiles("grouped", NG, [P, W // 2, 4], BF16)
-        swm = tiles("swm", 4, [P, W // 2, 4], BF16)
-        expo = tiles("expo", NE, [P, 2, 2, 2 * P], F32)
+        grouped = tiles("grouped", 2, [P, W, 4], BF16)
+        swm = tiles("swm", 2, [P, W, 4], BF16)
+        expo = tiles("expo", 2, [P, 2, 4, 2 * P], F32)
         sw = tiles("sw", NC, [P, 2, 4, 2 * P], BF16)
-        swn = tiles("swn", 2, [P, 2 * W], BF16)
+        swn = tiles("swn", 2, [P, W, 4], BF16)
         con_out = tiles("con_out", 3, [P, 2, W], F32)
         mom_out = tiles("mom_out", 4, [P, W], F32)
 
@@ -121,16 +125,27 @@ def tile_inverse_propensity_weighted_sums_s8_kernel(tc, x, beta, num, z, v_words
                     in_=v_scales[:, 4 * q : 4 * q + 4, :].rearrange("g r n -> r g n").bitcast(I32),
                 )
 
-        def interleave(copy, dst, src, half, c0, c1):
-            lo = half * W // 2
-            copy(
-                out=dst[:, c0:c1, :].rearrange("p (c i) t -> p c t i", i=4),
-                in_=src[:, :, lo + c0 : lo + c1].rearrange("p t (c i) -> p c t i", i=4),
-            )
+        def interleave(copy, dst, src, c0, c1):
+            if c1 > c0:
+                copy(
+                    out=dst[:, c0:c1, :].rearrange("p (c i) t -> p c t i", i=4),
+                    in_=src[:, :, c0:c1].rearrange("p t (c i) -> p c t i", i=4),
+                )
 
-        def quantize_half(codes, plane, half, values):
-            cols = slice(half * W // 2, (half + 1) * W // 2)
-            quantize(codes[:, cols], plane[:, cols], flat(values[:]))
+        def quantize_cols(codes, plane, values, h0, h1):
+            cols = slice(h0 * W // 2, h1 * W // 2)
+            quantize(codes[:, cols], plane[:, cols], flat(values[:, cols, :]))
+
+        def due(its, it):
+            found = []
+            for k in range(0, len(its), 2):
+                if its[k] == it and its[k + 1] == it:
+                    found.append((k // 2, 0, 2))
+                elif its[k] == it:
+                    found.append((k // 2, 0, 1))
+                elif its[k + 1] == it:
+                    found.append((k // 2, 1, 2))
+            return found
 
         def quantize(codes, plane, values):
             nc.vector.quantize_mx(out=codes.bitcast(FP8X4), scales=plane, in_=values)
@@ -138,8 +153,8 @@ def tile_inverse_propensity_weighted_sums_s8_kernel(tc, x, beta, num, z, v_words
         def flat(t3):
             return t3.rearrange("p a b -> p (a b)")
 
-        def x_transpose(i, it):
-            for tt in range(2):
+        def x_transpose(i, it, tts=(0, 1)):
+            for tt in tts:
                 acc = take(("x", i, tt), it)
                 words = x_rows(i, tt).bitcast(F32)
                 for c in range(2):
@@ -150,7 +165,7 @@ def tile_inverse_propensity_weighted_sums_s8_kernel(tc, x, beta, num, z, v_words
                         )
 
         def x_evict(i, tt):
-            nc.scalar.copy(
+            (nc.vector.tensor_copy if X_E[i] > tt else nc.scalar.copy)(
                 out=xt[i % 2][:, tt, :].bitcast(F32).rearrange("p (c m u) -> p c m u", c=2, u=2),
                 in_=held["x", i, tt][:].rearrange("p (c u m) -> p c m u", c=2, u=2),
             )
@@ -176,18 +191,18 @@ def tile_inverse_propensity_weighted_sums_s8_kernel(tc, x, beta, num, z, v_words
 
         def exp(s, tt):
             nc.scalar.activation(
-                out=expo[s % NE][:, :, tt, :].rearrange("p u (q e) -> p u q e", e=2),
+                out=expo[s // 2 % 2][:, :, 2 * (s % 2) + tt, :].rearrange("p u (q e) -> p u q e", e=2),
                 in_=held["e", s, tt][:].rearrange("p (q u e) -> p u q e", u=2, e=2),
                 func=ACT.Exp,
             )
 
-        def weigh(s):
-            unit, h = divmod(s, 2)
-            pairs = flat(num_raw[unit % 5][:, 2 * h : 2 * h + 2, :]).rearrange("p (a u e) -> p u a e", u=2, e=2)
+        def weigh(unit, h0, h1):
+            ts = slice(2 * h0, 2 * h1)
+            pairs = flat(num_raw[unit % 5][:, ts, :]).rearrange("p (a u e) -> p u a e", u=2, e=2)
             for u in range(2):
                 nc.vector.scalar_tensor_tensor(
-                    out=flat(sw[unit % NC][:, u, 2 * h : 2 * h + 2, :]).rearrange("p (a e) -> p a e", e=2),
-                    in0=flat(expo[s % NE][:, u, :, :]).rearrange("p (a e) -> p a e", e=2),
+                    out=flat(sw[unit % NC][:, u, ts, :]).rearrange("p (a e) -> p a e", e=2),
+                    in0=flat(expo[unit % 2][:, u, ts, :]).rearrange("p (a e) -> p a e", e=2),
                     scalar=1.0,
                     in1=pairs[:, u, :, :],
                     op0=ALU.add,
@@ -206,33 +221,32 @@ def tile_inverse_propensity_weighted_sums_s8_kernel(tc, x, beta, num, z, v_words
 
         def sw_evict(s):
             (nc.vector.tensor_copy if T_E[s] else nc.scalar.copy)(
-                out=swn[s % 2][:].bitcast(F32).rearrange("p (t m u) -> p t m u", t=2, u=2),
+                out=flat(swn[s // 2 % 2][:, 256 * (s % 2) : 256 * (s % 2 + 1), :]).bitcast(F32).rearrange("p (t m u) -> p t m u", t=2, u=2),
                 in_=held["t", s][:].rearrange("p (t u m) -> p t m u", t=2, u=2),
             )
 
-        def swn_quantize(s):
-            j, g = ORDER[s // 2]
-            i = 8 * g + 2 * j + s % 2
-            quantize(swn_codes[i][:], swn_plane[i][:], swn[s % 2][:])
+        def swn_quantize(unit, h0, h1):
+            j, g = ORDER[unit]
+            quantize_cols(swn_codes[4 * g + j], swn_plane[4 * g + j], swn[unit % 2], h0, h1)
 
-        def swm_interleave(unit, u):
+        def swm_interleave(unit, u0, u1):
             nc.vector.tensor_copy(
-                out=swm[(2 * unit + u) % 4][:].rearrange("p (c i) t -> p c t i", i=4),
-                in_=sw[unit % NC][:, u, :, :].rearrange("p t (c i) -> p c t i", i=4),
+                out=swm[unit % 2][:, 256 * u0 : 256 * u1, :].rearrange("p (u c i) t -> p u c t i", u=u1 - u0, i=4),
+                in_=sw[unit % NC][:, u0:u1, :, :].rearrange("p u t (c i) -> p u c t i", i=4),
             )
 
-        def swm_quantize(unit, u):
+        def swm_quantize(unit, u0, u1):
             j, g = ORDER[unit]
-            quantize_half(swm_codes[4 * g + j], swm_plane[4 * g + j], u, swm[(2 * unit + u) % 4])
+            quantize_cols(swm_codes[4 * g + j], swm_plane[4 * g + j], swm[unit % 2], u0, u1)
 
         def contrast(i, tt, it):
             acc = take(("c", i, tt), it)
             for g in range(2):
-                cols = slice(tt * P, (tt + 1) * P)
+                cols = slice((2 * (i % 2) + tt) * P, (2 * (i % 2) + tt + 1) * P)
                 nc.tensor.matmul_mx(
                     out=acc[:],
-                    lhsT=swn_codes[8 * g + i][:, cols].bitcast(FP8X4),
-                    lhsT_scale=swn_plane[8 * g + i][:, cols],
+                    lhsT=swn_codes[4 * g + i // 2][:, cols].bitcast(FP8X4),
+                    lhsT_scale=swn_plane[4 * g + i // 2][:, cols],
                     rhs=v_codes[:, g, :].bitcast(FP4X4),
                     rhs_scale=v_plane[:, g, :],
                     start=(g == 0),
@@ -266,77 +280,89 @@ def tile_inverse_propensity_weighted_sums_s8_kernel(tc, x, beta, num, z, v_words
             )
             nc.sync.dma_start(out=out_1[b * P : (b + 1) * P, g * W : (g + 1) * W], in_=mom_out[b][:])
 
-        load_beta(0, 0)
         nc.sync.dma_start(out=x_first[0][:], in_=x_v[0][:, 0, :])
+        load_beta(0, 0)
         load_beta(0, 1)
         nc.sync.dma_start(out=x_first[1][:], in_=x_v[0][:, 1, :])
         make_identity(nc, ident[:])
         nc.vector.memset(warm[:], 0.0)
         nc.scalar.activation(out=warm[:, 4:5], in_=warm[:, 0:1], func=ACT.Exp)
         nc.vector.memset(flat(v_plane[:]).bitcast(I32), 0)
-        for name in LOADS.split():
-            k = int(name[1:] or "0")
-            if name[0] == "x":
-                load_x(k)
-            elif name[0] == "b":
-                load_beta(k // 2, k % 2)
-            elif name[0] == "z":
-                load_z(k)
-            elif name[0] == "v":
-                load_v()
-            elif k < 5:
-                load_num(k)
         HW = W // 2
+        pending = LOADS.split()
+        done = set()
 
-        x_transpose(0, -2)
-        interleave(nc.vector.tensor_copy, grouped[0], beta_raw[0], 0, 0, HW)
-        interleave(nc.scalar.copy, grouped[1], beta_raw[0], 1, 0, HW)
+        def issue_loads():
+            while pending:
+                name = pending[0]
+                k = int(name[1:] or "0")
+                need = None
+                if name[0] == "x" and k > NX:
+                    need = "x%d" % (k - NX)
+                if name[0] == "n" and k >= 5:
+                    need = "n%d" % (k - 5)
+                if name[0] == "z" and k >= 2:
+                    need = "head"
+                if need is not None and need not in done:
+                    return
+                pending.pop(0)
+                if name[0] == "x":
+                    load_x(k)
+                elif name[0] == "b":
+                    load_beta(k // 2, k % 2)
+                elif name[0] == "z":
+                    load_z(k)
+                elif name[0] == "v":
+                    load_v()
+                else:
+                    load_num(k)
+
+        issue_loads()
+        x_transpose(0, -2, (0,))
         x_evict(0, 0)
-        quantize_half(beta_codes[0], beta_plane[0], 0, grouped[0])
-        interleave(nc.vector.tensor_copy, grouped[2], beta_raw[1], 0, 0, HW)
-        quantize_half(beta_codes[0], beta_plane[0], 1, grouped[1])
-        interleave(nc.vector.tensor_copy, grouped[3], beta_raw[1], 1, 0, HW)
+        interleave(nc.vector.tensor_copy, grouped[0], beta_raw[0], 0, HEAD[0])
+        interleave(nc.scalar.copy, grouped[0], beta_raw[0], HEAD[0], W)
+        quantize(x_codes[0][:, :HW], x_plane[0][:, :HW], xt[0][:, 0, :])
+        quantize_cols(beta_codes[0], beta_plane[0], grouped[0], 0, 2)
+        interleave(nc.vector.tensor_copy, grouped[1], beta_raw[1], 0, HEAD[1])
+        interleave(nc.scalar.copy, grouped[1], beta_raw[1], HEAD[1], W)
+        x_transpose(0, -2, (1,))
         x_evict(0, 1)
-        quantize_half(beta_codes[1], beta_plane[1], 0, grouped[2])
         x_transpose(1, -1)
-        x_quantize(0)
-        quantize_half(beta_codes[1], beta_plane[1], 1, grouped[3])
+        quantize_cols(beta_codes[1], beta_plane[1], grouped[1], 0, 2)
+        quantize(x_codes[0][:, HW:], x_plane[0][:, HW:], xt[0][:, 1, :])
         x_evict(1, 0)
         x_evict(1, 1)
-
-        il_it = {}
-        for k in range(16):
-            il_it[k // 2, k % 2] = IL_IT[k]
+        done.add("head")
+        done.add("x1")
+        issue_loads()
+        side = [(beta_raw[2 + c], beta_codes[2 + c], beta_plane[2 + c]) for c in range(2)]
+        side = side + [(z_raw[j], z_codes[j], z_plane[j]) for j in range(4)]
+        side_it, side_v = B_IT + Z_IT, B_V + Z_V
         t_it = T_IT
         for it in range(STEPS + 4):
-            if 0 <= it - 1 < STEPS:
-                weigh(it - 1)
-                if (it - 1) % 2 == 1 and 5 <= (it - 1) // 2 + 5 < 8:
-                    load_num((it - 1) // 2 + 5)
-            for k in range(4):
-                if B_IT[k] + 1 == it:
-                    quantize_half(beta_codes[2 + k // 2], beta_plane[2 + k // 2], k % 2, grouped[k % NG])
-            for k in range(8):
-                if Z_IT[k] + 1 == it:
-                    quantize_half(z_codes[k // 2], z_plane[k // 2], k % 2, grouped[k % NG])
-            for i in range(1, 8):
-                if X_IT[i] + 1 == it:
-                    x_quantize(i)
-            for key in il_it:
-                if il_it[key] + 1 == it:
-                    swm_quantize(*key)
-            for s in range(STEPS):
-                if t_it[s] + 1 == it:
-                    swn_quantize(s)
-            for key in il_it:
-                if il_it[key] == it:
-                    swm_interleave(*key)
-            for k in range(4):
-                if B_IT[k] == it and B_V[k] > 0:
-                    interleave(nc.vector.tensor_copy, grouped[k % NG], beta_raw[2 + k // 2], k % 2, 0, B_V[k])
-            for k in range(8):
-                if Z_IT[k] == it and Z_V[k] > 0:
-                    interleave(nc.vector.tensor_copy, grouped[k % NG], z_raw[k // 2], k % 2, 0, Z_V[k])
+            for part in ["sqi", "qsi", "siq", "isq", "qis", "iqs"][V_ORD[it]]:
+                if part == "s":
+                    for unit, h0, h1 in due(S_IT, it):
+                        weigh(unit, h0, h1)
+                        if h1 == 2:
+                            done.add("n%d" % unit)
+                if part == "q":
+                    for i in range(1, 8):
+                        if X_IT[i] + 1 == it:
+                            x_quantize(i)
+                    for k, h0, h1 in due(side_it, it - 1):
+                        quantize_cols(side[k][1], side[k][2], grouped[k % 2], h0, h1)
+                    for job in due(IL_IT, it - 1):
+                        swm_quantize(*job)
+                    for job in due(T_IT, it - 1):
+                        swn_quantize(*job)
+                if part == "i":
+                    for job in due(IL_IT, it):
+                        swm_interleave(*job)
+                    for k, h0, h1 in due(side_it, it):
+                        share = sum(side_v[2 * k + h0 : 2 * k + h1])
+                        interleave(nc.vector.tensor_copy, grouped[k % 2], side[k][0], h0 * HW, h0 * HW + share)
             if it < STEPS:
                 eta(it, 0)
                 eta(it, 1)
@@ -366,12 +392,11 @@ def tile_inverse_propensity_weighted_sums_s8_kernel(tc, x, beta, num, z, v_words
                             x_transpose(i, it)
                             x_evict(i, 0)
                             x_evict(i, 1)
-            for k in range(4):
-                if B_IT[k] == it and B_V[k] < HW:
-                    interleave(nc.scalar.copy, grouped[k % NG], beta_raw[2 + k // 2], k % 2, B_V[k], HW)
-            for k in range(8):
-                if Z_IT[k] == it and Z_V[k] < HW:
-                    interleave(nc.scalar.copy, grouped[k % NG], z_raw[k // 2], k % 2, Z_V[k], HW)
+                            done.add("x%d" % i)
+            for k, h0, h1 in due(side_it, it):
+                share = sum(side_v[2 * k + h0 : 2 * k + h1])
+                interleave(nc.scalar.copy, grouped[k % 2], side[k][0], h0 * HW + share, h1 * HW)
+            issue_loads()
             for g in range(2):
                 if MOM_IT[4 * g + 3] == it:
                     for b in range(4):

@@ -3,8 +3,8 @@ from contextlib import ExitStack
 import concourse.mybir as mybir
 from concourse.masks import make_identity
 
-M, K, N, R, PZ = 2048, 1024, 1024, 512, 512
-FLOPS = 2 * M * K * N + 2 * M * N * R + 2 * PZ * M * N
+M, K, N, R, Z_COLS = 2048, 1024, 1024, 512, 512
+FLOPS = 2 * M * K * N + 2 * M * N * R + 2 * Z_COLS * M * N
 
 F32 = mybir.dt.float32
 BF16 = mybir.dt.bfloat16
@@ -18,33 +18,22 @@ ACT = mybir.ActivationFunctionType
 
 P = 128
 W = 512
-STEPS = 16
-ORDER = [(0, 0), (1, 0), (0, 1), (2, 0), (3, 0), (1, 1), (2, 1), (3, 1)]
-X_IT = [-2,-1,0,1,3,4,5,6]
-CON_IT = [8,9,14,15,16,17,17,19]
-MOM_IT = [9,10,11,13,14,15,17,18]
-MOM_OUT_V = [0, 1]
-B_IT = [1,1,2,2]
-Z_IT = [4,5,6,7,8,9,10,11]
-Z_V = [128,128,128,128,64,64,64,64]
-LOADS = "x1 n0 x2 b2 x3 n1 b3 x4 n2 z0 x5 v n3 z1 x6 x7 n4 z2 z3 n5 n6 n7"
-SWT_LAG = 1
-TPAIR = 99
-CON_V = 16
-IL_IT = [2,3,4,5,6,7,8,9,10,11,12,13,14,15,16,16]
-CON_E = [0,0,0,0,0,0,0,1]
-T_IT = [2,3,4,5,6,7,8,9,10,11,12,13,14,15,15,16]
-S_IT = [1,2,3,4,5,6,7,8,9,10,11,12,13,14,15,16]
-V_ORD = [0,0,0,0,0,0,0,0,0,0,0,0,0,0,0,0,0,0,0,0]
-X_E = [0,0,0,0,0,0,0,0]
-NX = 5
-T_E = [0,0,0,0,0,0,0,0,0,0,0,0,0,0,0,0]
-B_V = [192,192,192,192]
-MO_E = [1,0,1,0,0,1,0,1]
-PE_ORD = [4,4,4,4,4,4,4,4,4,4,4,4,4,4,4,4,4,4,4,4]
-HEAD = [320,320]
-NC = 3
-NG = 4
+HW = W // 2
+GROUPS, HALVES = M // W, N // W
+PAIRS = 2 * GROUPS
+STEPS = 2 * GROUPS * HALVES
+
+UNITS = [(0, 0), (1, 0), (0, 1), (2, 0), (3, 0), (1, 1), (2, 1), (3, 1)]
+
+X_LEAD = 3
+TURN_LAG = 2
+USE_LAG = 2
+BETA_ROUND = 1
+Z_ROUND = 4
+
+SHARE_EARLY, SHARE_LATE = 0.75, 0.25
+
+X_TILES, NUM_TILES, SW_TILES, CONTRAST_TILES = 5, 5, 3, 3
 
 
 def tile_inverse_propensity_weighted_sums_s8_kernel(tc, x, beta, num, z, v_words, v_scales, out_0, out_1):
@@ -57,228 +46,235 @@ def tile_inverse_propensity_weighted_sums_s8_kernel(tc, x, beta, num, z, v_words
         def tiles(name, count, shape, dtype):
             return [sb.tile(shape, dtype, name="%s%d" % (name, i), align_bytes=64) for i in range(count)]
 
+        def flat(view):
+            return view.rearrange("p a b -> p (a b)")
+
+        unit_of = {key: unit for unit, key in enumerate(UNITS)}
+        last_unit = len(UNITS) - 1
+        x_round = {}
+        for pair in range(2, PAIRS):
+            first_step = 2 * unit_of[pair // 2, 0] + pair % 2
+            x_round[pair] = max(first_step - X_LEAD, pair - 2)
+        turn_round = [s + TURN_LAG - (1 if s // 2 == last_unit else 0) for s in range(STEPS)]
+        weave_round = [2 * unit + (2 if unit == last_unit else 3) for unit in range(len(UNITS))]
+        z_round = [Z_ROUND + job for job in range(2 * GROUPS)]
+        moment_round = {}
+        previous = 0
+        for g in range(HALVES):
+            for j in range(GROUPS):
+                ready = max(weave_round[unit_of[j, g]], z_round[2 * j + 1]) + USE_LAG
+                previous = max(ready, previous + 1)
+                moment_round[g, j] = previous
+        contrast_round = [turn_round[2 * unit_of[pair // 2, 1] + pair % 2] + USE_LAG for pair in range(PAIRS)]
+        contrast_round[-1] = previous + 1
+        rounds = contrast_round[-1] + 1
+
         bank = [ps.tile([P, W], F32, name="bank%d" % i) for i in range(8)]
+        moment_bank = bank[4:]
         held = {}
-        ring = [0]
+        cursor = [0]
 
-        def take(key, it):
-            size = 8 if it < MOM_IT[0] else 4
-            held[key] = bank[ring[0] % size]
-            ring[0] = (ring[0] + 1) % size
+        def take_bank(key, now):
+            count = 8 if now < moment_round[0, 0] else 4
+            held[key] = bank[cursor[0] % count]
+            cursor[0] = (cursor[0] + 1) % count
             return held[key]
-
 
         ident = sb.tile([P, P], F32, name="ident", align_bytes=64)
         warm = sb.tile([P, 8], F32, name="warm", align_bytes=64)
         x_first = tiles("x_first", 2, [P, K], BF16)
-        x_raw = tiles("x_raw", NX, [P, 2, K], BF16)
+        x_raw = tiles("x_raw", X_TILES, [P, 2, K], BF16)
         beta_raw = tiles("beta_raw", 4, [P, 4, W], BF16)
         z_raw = tiles("z_raw", 2, [P, 4, W], BF16) + beta_raw[:2]
-        num_raw = tiles("num_raw", 5, [P, 4, W], BF16)
-        v_codes = sb.tile([P, 2, 2 * W], U8, name="v_codes", align_bytes=64)
-        v_plane = sb.tile([P, 2, W], U8, name="v_plane", align_bytes=64)
+        num_raw = tiles("num_raw", NUM_TILES, [P, 4, W], BF16)
+        v_codes = sb.tile([P, HALVES, 2 * R], U8, name="v_codes", align_bytes=64)
+        v_plane = sb.tile([P, HALVES, R], U8, name="v_plane", align_bytes=64)
 
-        x_codes, x_plane = tiles("x_codes", 8, [P, W], U32), tiles("x_plane", 8, [P, W], U8)
+        x_codes, x_plane = tiles("x_codes", PAIRS, [P, W], U32), tiles("x_plane", PAIRS, [P, W], U8)
         beta_codes, beta_plane = tiles("beta_codes", 4, [P, W], U32), tiles("beta_plane", 4, [P, W], U8)
-        z_codes, z_plane = tiles("z_codes", 4, [P, W], U32), tiles("z_plane", 4, [P, W], U8)
+        z_codes, z_plane = tiles("z_codes", GROUPS, [P, W], U32), tiles("z_plane", GROUPS, [P, W], U8)
         swm_codes, swm_plane = tiles("swm_codes", 8, [P, W], U32), tiles("swm_plane", 8, [P, W], U8)
-        swn_codes, swn_plane = tiles("swn_codes", 8, [P, W], U32), tiles("swn_plane", 8, [P, W], U8)
+        swc_codes, swc_plane = tiles("swc_codes", 8, [P, W], U32), tiles("swc_plane", 8, [P, W], U8)
 
-        xt = tiles("xt", 2, [P, 2, 2 * W], BF16)
-        grouped = tiles("grouped", 2, [P, W, 4], BF16)
-        swm = tiles("swm", 2, [P, W, 4], BF16)
-        expo = tiles("expo", 2, [P, 2, 4, 2 * P], F32)
-        sw = tiles("sw", NC, [P, 2, 4, 2 * P], BF16)
-        swn = tiles("swn", 2, [P, W, 4], BF16)
-        con_out = tiles("con_out", 3, [P, 2, W], F32)
-        mom_out = tiles("mom_out", 4, [P, W], F32)
+        x_words = tiles("x_words", 2, [P, 2, 2 * W], BF16)
+        side_words = tiles("side_words", 2, [P, W, 4], BF16)
+        swm_words = tiles("swm_words", 2, [P, W, 4], BF16)
+        exp_eta = tiles("exp_eta", 2, [P, 2, 4, HW], F32)
+        sw = tiles("sw", SW_TILES, [P, 2, 4, HW], BF16)
+        swc_words = tiles("swc_words", 2, [P, W, 4], BF16)
+        contrast_out = tiles("contrast_out", CONTRAST_TILES, [P, 2, R], F32)
+        moment_out = tiles("moment_out", 4, [P, W], F32)
 
         x_v = x.rearrange("(j p t) k -> j p t k", p=P, t=4)
         num_v = num.rearrange("(j p t) n -> j p t n", p=P, t=4)
         z_v = z.rearrange("(j p t) c -> j p t c", p=P, t=4)
         beta_v = beta.rearrange("(c p t) n -> c p t n", p=P, t=4)
-        out0_v = out_0.rearrange("(j p t) r -> j p t r", p=P, t=4)
+        contrast_v = out_0.rearrange("(j p t) r -> j p t r", p=P, t=4)
 
-        def x_rows(i, tt):
-            if i == 0:
-                return x_first[tt][:]
-            return x_raw[(i - 1) % len(x_raw)][:, tt, :]
-
-        def load_x(i):
-            nc.sync.dma_start(out=x_raw[(i - 1) % len(x_raw)][:], in_=x_v[i // 2][:, 2 * (i % 2) : 2 * (i % 2) + 2, :])
+        def load_x(pair):
+            j, h = divmod(pair, 2)
+            nc.sync.dma_start(out=x_raw[(pair - 1) % X_TILES][:], in_=x_v[j][:, 2 * h : 2 * h + 2, :])
 
         def load_beta(g, c):
             nc.sync.dma_start(out=beta_raw[2 * g + c][:], in_=beta_v[c][:, :, g * W : (g + 1) * W])
 
-        def load_num(u):
-            j, g = ORDER[u]
-            nc.sync.dma_start(out=num_raw[u % 5][:], in_=num_v[j][:, :, g * W : (g + 1) * W])
+        def load_num(unit):
+            j, g = UNITS[unit]
+            nc.sync.dma_start(out=num_raw[unit % NUM_TILES][:], in_=num_v[j][:, :, g * W : (g + 1) * W])
 
         def load_z(j):
             nc.sync.dma_start(out=z_raw[j][:], in_=z_v[j])
 
         def load_v():
             nc.sync.dma_start(out=v_codes[:].bitcast(I32), in_=v_words.rearrange("g p b -> p g b").bitcast(I32))
-            for q in range(4):
+            for quad in range(4):
                 nc.sync.dma_start(
-                    out=v_plane[32 * q : 32 * q + 4, :, :].bitcast(I32),
-                    in_=v_scales[:, 4 * q : 4 * q + 4, :].rearrange("g r n -> r g n").bitcast(I32),
+                    out=v_plane[32 * quad : 32 * quad + 4, :, :].bitcast(I32),
+                    in_=v_scales[:, 4 * quad : 4 * quad + 4, :].rearrange("g r n -> r g n").bitcast(I32),
                 )
 
-        def interleave(copy, dst, src, c0, c1):
-            if c1 > c0:
-                copy(
-                    out=dst[:, c0:c1, :].rearrange("p (c i) t -> p c t i", i=4),
-                    in_=src[:, :, c0:c1].rearrange("p t (c i) -> p c t i", i=4),
-                )
-
-        def quantize_cols(codes, plane, values, h0, h1):
-            cols = slice(h0 * W // 2, h1 * W // 2)
-            quantize(codes[:, cols], plane[:, cols], flat(values[:, cols, :]))
-
-        def due(its, it):
-            found = []
-            for k in range(0, len(its), 2):
-                if its[k] == it and its[k + 1] == it:
-                    found.append((k // 2, 0, 2))
-                elif its[k] == it:
-                    found.append((k // 2, 0, 1))
-                elif its[k + 1] == it:
-                    found.append((k // 2, 1, 2))
-            return found
+        def interleave(copy, words, rows, c0, c1):
+            copy(
+                out=words[:, c0:c1, :].rearrange("p (c i) t -> p c t i", i=4),
+                in_=rows[:, :, c0:c1].rearrange("p t (c i) -> p c t i", i=4),
+            )
 
         def quantize(codes, plane, values):
             nc.vector.quantize_mx(out=codes.bitcast(FP8X4), scales=plane, in_=values)
 
-        def flat(t3):
-            return t3.rearrange("p a b -> p (a b)")
+        def quantize_columns(codes, plane, words, c0, c1):
+            quantize(codes[:, c0:c1], plane[:, c0:c1], flat(words[:, c0:c1, :]))
 
-        def x_transpose(i, it, tts=(0, 1)):
-            for tt in tts:
-                acc = take(("x", i, tt), it)
-                words = x_rows(i, tt).bitcast(F32)
-                for c in range(2):
-                    for u in range(2):
-                        col = (2 * c + u) * P
-                        nc.tensor.transpose(
-                            acc[:, col : col + P], words[:, 256 * c + u : 256 * (c + 1) : 2], ident[:]
-                        )
+        def x_transpose(pair, slot, now):
+            rows = x_first[slot][:] if pair == 0 else x_raw[(pair - 1) % X_TILES][:, slot, :]
+            packed = rows.bitcast(F32)
+            acc = take_bank(("x", pair, slot), now)
+            for c in range(2):
+                for u in range(2):
+                    col = (2 * c + u) * P
+                    nc.tensor.transpose(acc[:, col : col + P], packed[:, HW * c + u : HW * (c + 1) : 2], ident[:])
 
-        def x_evict(i, tt):
-            (nc.vector.tensor_copy if X_E[i] > tt else nc.scalar.copy)(
-                out=xt[i % 2][:, tt, :].bitcast(F32).rearrange("p (c m u) -> p c m u", c=2, u=2),
-                in_=held["x", i, tt][:].rearrange("p (c u m) -> p c m u", c=2, u=2),
+        def x_evict(pair, slot):
+            nc.scalar.copy(
+                out=x_words[pair % 2][:, slot, :].bitcast(F32).rearrange("p (c m u) -> p c m u", c=2, u=2),
+                in_=held["x", pair, slot][:].rearrange("p (c u m) -> p c m u", c=2, u=2),
             )
 
-        def x_quantize(i):
-            quantize(x_codes[i][:], x_plane[i][:], flat(xt[i % 2][:]))
-
-        def eta(s, tt):
-            j, g = ORDER[s // 2]
-            i = 2 * j + s % 2
-            acc = take(("e", s, tt), s)
+        def eta(step, slot):
+            j, g = UNITS[step // 2]
+            pair = 2 * j + step % 2
+            acc = take_bank(("eta", step, slot), step)
             for c in range(2):
-                cols = slice((2 * tt + c) * P, (2 * tt + c + 1) * P)
+                cols = slice((2 * slot + c) * P, (2 * slot + c + 1) * P)
                 nc.tensor.matmul_mx(
                     out=acc[:],
-                    lhsT=x_codes[i][:, cols].bitcast(FP8X4),
-                    lhsT_scale=x_plane[i][:, cols],
+                    lhsT=x_codes[pair][:, cols].bitcast(FP8X4),
+                    lhsT_scale=x_plane[pair][:, cols],
                     rhs=beta_codes[2 * g + c][:].bitcast(FP8X4),
                     rhs_scale=beta_plane[2 * g + c][:],
                     start=(c == 0),
                     stop=(c == 1),
                 )
 
-        def exp(s, tt):
+        def exponential(step, slot):
+            unit, h = divmod(step, 2)
             nc.scalar.activation(
-                out=expo[s // 2 % 2][:, :, 2 * (s % 2) + tt, :].rearrange("p u (q e) -> p u q e", e=2),
-                in_=held["e", s, tt][:].rearrange("p (q u e) -> p u q e", u=2, e=2),
+                out=exp_eta[unit % 2][:, :, 2 * h + slot, :].rearrange("p u (q e) -> p u q e", e=2),
+                in_=held["eta", step, slot][:].rearrange("p (q u e) -> p u q e", u=2, e=2),
                 func=ACT.Exp,
             )
 
-        def weigh(unit, h0, h1):
-            ts = slice(2 * h0, 2 * h1)
-            pairs = flat(num_raw[unit % 5][:, ts, :]).rearrange("p (a u e) -> p u a e", u=2, e=2)
+        def weigh(step):
+            unit, h = divmod(step, 2)
+            slots = slice(2 * h, 2 * h + 2)
+            numerators = flat(num_raw[unit % NUM_TILES][:, slots, :]).rearrange("p (a u e) -> p u a e", u=2, e=2)
             for u in range(2):
                 nc.vector.scalar_tensor_tensor(
-                    out=flat(sw[unit % NC][:, u, ts, :]).rearrange("p (a e) -> p a e", e=2),
-                    in0=flat(expo[unit % 2][:, u, ts, :]).rearrange("p (a e) -> p a e", e=2),
+                    out=flat(sw[unit % SW_TILES][:, u, slots, :]).rearrange("p (a e) -> p a e", e=2),
+                    in0=flat(exp_eta[unit % 2][:, u, slots, :]).rearrange("p (a e) -> p a e", e=2),
                     scalar=1.0,
-                    in1=pairs[:, u, :, :],
+                    in1=numerators[:, u, :, :],
                     op0=ALU.add,
                     op1=ALU.mult,
                 )
 
-        def sw_transpose(s, it):
-            acc = take(("t", s), it)
-            unit, h = divmod(s, 2)
-            for tt in range(2):
+        def sw_turn(step, now):
+            unit, h = divmod(step, 2)
+            acc = take_bank(("sw", step), now)
+            for slot in range(2):
                 for u in range(2):
-                    col = (2 * tt + u) * P
-                    nc.tensor.transpose(
-                        acc[:, col : col + P], sw[unit % NC][:, u, 2 * h + tt, :].bitcast(F32), ident[:]
-                    )
-
-        def sw_evict(s):
-            (nc.vector.tensor_copy if T_E[s] else nc.scalar.copy)(
-                out=flat(swn[s // 2 % 2][:, 256 * (s % 2) : 256 * (s % 2 + 1), :]).bitcast(F32).rearrange("p (t m u) -> p t m u", t=2, u=2),
-                in_=held["t", s][:].rearrange("p (t u m) -> p t m u", t=2, u=2),
+                    col = (2 * slot + u) * P
+                    packed = sw[unit % SW_TILES][:, u, 2 * h + slot, :].bitcast(F32)
+                    nc.tensor.transpose(acc[:, col : col + P], packed, ident[:])
+            nc.scalar.copy(
+                out=flat(swc_words[unit % 2][:, HW * h : HW * (h + 1), :]).bitcast(F32).rearrange("p (a m u) -> p a m u", a=2, u=2),
+                in_=acc[:].rearrange("p (a u m) -> p a m u", a=2, u=2),
             )
 
-        def swn_quantize(unit, h0, h1):
-            j, g = ORDER[unit]
-            quantize_cols(swn_codes[4 * g + j], swn_plane[4 * g + j], swn[unit % 2], h0, h1)
+        def swc_quantize(unit, h0, h1):
+            j, g = UNITS[unit]
+            quantize_columns(swc_codes[4 * g + j], swc_plane[4 * g + j], swc_words[unit % 2], HW * h0, HW * h1)
 
-        def swm_interleave(unit, u0, u1):
+        def sw_weave(unit):
             nc.vector.tensor_copy(
-                out=swm[unit % 2][:, 256 * u0 : 256 * u1, :].rearrange("p (u c i) t -> p u c t i", u=u1 - u0, i=4),
-                in_=sw[unit % NC][:, u0:u1, :, :].rearrange("p u t (c i) -> p u c t i", i=4),
+                out=swm_words[unit % 2][:].rearrange("p (u c i) t -> p u c t i", u=2, i=4),
+                in_=sw[unit % SW_TILES][:].rearrange("p u t (c i) -> p u c t i", i=4),
             )
 
-        def swm_quantize(unit, u0, u1):
-            j, g = ORDER[unit]
-            quantize_cols(swm_codes[4 * g + j], swm_plane[4 * g + j], swm[unit % 2], u0, u1)
+        def swm_quantize(unit):
+            j, g = UNITS[unit]
+            quantize_columns(swm_codes[4 * g + j], swm_plane[4 * g + j], swm_words[unit % 2], 0, W)
 
-        def contrast(i, tt, it):
-            acc = take(("c", i, tt), it)
-            for g in range(2):
-                cols = slice((2 * (i % 2) + tt) * P, (2 * (i % 2) + tt + 1) * P)
+        def contrast(pair, now):
+            j, h = divmod(pair, 2)
+            result = contrast_out[pair % CONTRAST_TILES]
+            for slot in range(2):
+                acc = take_bank(("contrast", pair, slot), now)
+                cols = slice((2 * h + slot) * P, (2 * h + slot + 1) * P)
+                for g in range(HALVES):
+                    nc.tensor.matmul_mx(
+                        out=acc[:],
+                        lhsT=swc_codes[4 * g + j][:, cols].bitcast(FP8X4),
+                        lhsT_scale=swc_plane[4 * g + j][:, cols],
+                        rhs=v_codes[:, g, :].bitcast(FP4X4),
+                        rhs_scale=v_plane[:, g, :],
+                        start=(g == 0),
+                        stop=(g == HALVES - 1),
+                    )
+                copy = nc.vector.tensor_copy if (pair, slot) == (PAIRS - 1, 1) else nc.scalar.copy
+                copy(out=result[:, slot, :], in_=acc[:])
+            nc.sync.dma_start(out=contrast_v[j][:, 2 * h : 2 * h + 2, :], in_=result[:])
+
+        def moment_pass(g, j):
+            for b in range(4):
+                cols = slice(b * P, (b + 1) * P)
                 nc.tensor.matmul_mx(
-                    out=acc[:],
-                    lhsT=swn_codes[4 * g + i // 2][:, cols].bitcast(FP8X4),
-                    lhsT_scale=swn_plane[4 * g + i // 2][:, cols],
-                    rhs=v_codes[:, g, :].bitcast(FP4X4),
-                    rhs_scale=v_plane[:, g, :],
-                    start=(g == 0),
-                    stop=(g == 1),
-                )
-
-        def contrast_evict(copy, i, tt):
-            copy(out=con_out[i % 3][:, tt, :], in_=held["c", i, tt][:])
-
-        def contrast_store(i):
-            j, h = divmod(i, 2)
-            nc.sync.dma_start(out=out0_v[j][:, 2 * h : 2 * h + 2, :], in_=con_out[i % 3][:])
-
-        def moment(g, b, acc, groups):
-            cols = slice(b * P, (b + 1) * P)
-            for j in groups:
-                nc.tensor.matmul_mx(
-                    out=acc[:],
+                    out=moment_bank[b][:],
                     lhsT=z_codes[j][:, cols].bitcast(FP8X4),
                     lhsT_scale=z_plane[j][:, cols],
                     rhs=swm_codes[4 * g + j][:].bitcast(FP8X4),
                     rhs_scale=swm_plane[4 * g + j][:],
                     start=(j == 0),
-                    stop=(j == 3),
+                    stop=(j == GROUPS - 1),
                 )
 
-        def moment_out(copy, g, b, acc):
-            copy(
-                out=mom_out[b][:].rearrange("p (q u e) -> p q u e", u=2, e=2),
-                in_=acc[:].rearrange("p (u q e) -> p q u e", u=2, e=2),
-            )
-            nc.sync.dma_start(out=out_1[b * P : (b + 1) * P, g * W : (g + 1) * W], in_=mom_out[b][:])
+        def moment_store(g):
+            for b in range(4):
+                copy = nc.vector.tensor_copy if b % 2 else nc.scalar.copy
+                copy(
+                    out=moment_out[b][:].rearrange("p (q u e) -> p q u e", u=2, e=2),
+                    in_=moment_bank[b][:].rearrange("p (u q e) -> p q u e", u=2, e=2),
+                )
+                nc.sync.dma_start(out=out_1[b * P : (b + 1) * P, g * W : (g + 1) * W], in_=moment_out[b][:])
+
+        side = {}
+        for c in range(2):
+            job = (beta_raw[2 + c], beta_codes[2 + c], beta_plane[2 + c], side_words[c], 0, int(SHARE_EARLY * W), W)
+            side[BETA_ROUND + c] = job
+        for job_index in range(2 * GROUPS):
+            j, part = divmod(job_index, 2)
+            split = HW * part + int((SHARE_EARLY if j < 2 else SHARE_LATE) * HW)
+            side[z_round[job_index]] = (z_raw[j], z_codes[j], z_plane[j], side_words[j % 2], HW * part, split, HW * (part + 1))
 
         nc.sync.dma_start(out=x_first[0][:], in_=x_v[0][:, 0, :])
         load_beta(0, 0)
@@ -288,116 +284,91 @@ def tile_inverse_propensity_weighted_sums_s8_kernel(tc, x, beta, num, z, v_words
         nc.vector.memset(warm[:], 0.0)
         nc.scalar.activation(out=warm[:, 4:5], in_=warm[:, 0:1], func=ACT.Exp)
         nc.vector.memset(flat(v_plane[:]).bitcast(I32), 0)
-        HW = W // 2
-        pending = LOADS.split()
-        done = set()
+        load_x(1)
+        load_num(0)
+        load_x(2)
+        load_beta(1, 0)
+        load_x(3)
+        load_num(1)
+        load_beta(1, 1)
+        load_x(4)
+        load_x(5)
+        load_num(2)
+        load_z(0)
 
-        def issue_loads():
-            while pending:
-                name = pending[0]
-                k = int(name[1:] or "0")
-                need = None
-                if name[0] == "x" and k > NX:
-                    need = "x%d" % (k - NX)
-                if name[0] == "n" and k >= 5:
-                    need = "n%d" % (k - 5)
-                if name[0] == "z" and k >= 2:
-                    need = "head"
-                if need is not None and need not in done:
-                    return
-                pending.pop(0)
-                if name[0] == "x":
-                    load_x(k)
-                elif name[0] == "b":
-                    load_beta(k // 2, k % 2)
-                elif name[0] == "z":
-                    load_z(k)
-                elif name[0] == "v":
-                    load_v()
-                else:
-                    load_num(k)
-
-        issue_loads()
-        x_transpose(0, -2, (0,))
+        split = int(SHARE_EARLY * W)
+        x_transpose(0, 0, -1)
         x_evict(0, 0)
-        interleave(nc.vector.tensor_copy, grouped[0], beta_raw[0], 0, HEAD[0])
-        interleave(nc.scalar.copy, grouped[0], beta_raw[0], HEAD[0], W)
-        quantize(x_codes[0][:, :HW], x_plane[0][:, :HW], xt[0][:, 0, :])
-        quantize_cols(beta_codes[0], beta_plane[0], grouped[0], 0, 2)
-        interleave(nc.vector.tensor_copy, grouped[1], beta_raw[1], 0, HEAD[1])
-        interleave(nc.scalar.copy, grouped[1], beta_raw[1], HEAD[1], W)
-        x_transpose(0, -2, (1,))
+        interleave(nc.vector.tensor_copy, side_words[0], beta_raw[0], 0, split)
+        interleave(nc.scalar.copy, side_words[0], beta_raw[0], split, W)
+        quantize(x_codes[0][:, :HW], x_plane[0][:, :HW], x_words[0][:, 0, :])
+        quantize_columns(beta_codes[0], beta_plane[0], side_words[0], 0, W)
+        interleave(nc.vector.tensor_copy, side_words[1], beta_raw[1], 0, split)
+        interleave(nc.scalar.copy, side_words[1], beta_raw[1], split, W)
+        x_transpose(0, 1, -1)
         x_evict(0, 1)
-        x_transpose(1, -1)
-        quantize_cols(beta_codes[1], beta_plane[1], grouped[1], 0, 2)
-        quantize(x_codes[0][:, HW:], x_plane[0][:, HW:], xt[0][:, 1, :])
+        x_transpose(1, 0, -1)
+        x_transpose(1, 1, -1)
+        quantize_columns(beta_codes[1], beta_plane[1], side_words[1], 0, W)
+        quantize(x_codes[0][:, HW:], x_plane[0][:, HW:], x_words[0][:, 1, :])
         x_evict(1, 0)
         x_evict(1, 1)
-        done.add("head")
-        done.add("x1")
-        issue_loads()
-        side = [(beta_raw[2 + c], beta_codes[2 + c], beta_plane[2 + c]) for c in range(2)]
-        side = side + [(z_raw[j], z_codes[j], z_plane[j]) for j in range(4)]
-        side_it, side_v = B_IT + Z_IT, B_V + Z_V
-        t_it = T_IT
-        for it in range(STEPS + 4):
-            for part in ["sqi", "qsi", "siq", "isq", "qis", "iqs"][V_ORD[it]]:
-                if part == "s":
-                    for unit, h0, h1 in due(S_IT, it):
-                        weigh(unit, h0, h1)
-                        if h1 == 2:
-                            done.add("n%d" % unit)
-                if part == "q":
-                    for i in range(1, 8):
-                        if X_IT[i] + 1 == it:
-                            x_quantize(i)
-                    for k, h0, h1 in due(side_it, it - 1):
-                        quantize_cols(side[k][1], side[k][2], grouped[k % 2], h0, h1)
-                    for job in due(IL_IT, it - 1):
-                        swm_quantize(*job)
-                    for job in due(T_IT, it - 1):
-                        swn_quantize(*job)
-                if part == "i":
-                    for job in due(IL_IT, it):
-                        swm_interleave(*job)
-                    for k, h0, h1 in due(side_it, it):
-                        share = sum(side_v[2 * k + h0 : 2 * k + h1])
-                        interleave(nc.vector.tensor_copy, grouped[k % 2], side[k][0], h0 * HW, h0 * HW + share)
-            if it < STEPS:
-                eta(it, 0)
-                eta(it, 1)
-                exp(it, 0)
-                exp(it, 1)
-            for part in ["mct", "cmt", "tcm", "tmc", "ctm", "mtc"][PE_ORD[it]]:
-                if part == "m":
-                    for k in range(8):
-                        if MOM_IT[k] == it:
-                            for b in range(4):
-                                moment(k // 4, b, bank[4 + b], range(k % 4, k % 4 + 1))
-                if part == "c":
-                    for i in range(8):
-                        if CON_IT[i] == it:
-                            contrast(i, 0, it)
-                            contrast_evict(nc.scalar.copy, i, 0)
-                            contrast(i, 1, it)
-                            contrast_evict(nc.scalar.copy if CON_E[i] == 0 else nc.vector.tensor_copy, i, 1)
-                            contrast_store(i)
-                if part == "t":
-                    for s in range(STEPS):
-                        if t_it[s] == it:
-                            sw_transpose(s, it)
-                            sw_evict(s)
-                    for i in range(2, 8):
-                        if X_IT[i] == it:
-                            x_transpose(i, it)
-                            x_evict(i, 0)
-                            x_evict(i, 1)
-                            done.add("x%d" % i)
-            for k, h0, h1 in due(side_it, it):
-                share = sum(side_v[2 * k + h0 : 2 * k + h1])
-                interleave(nc.scalar.copy, grouped[k % 2], side[k][0], h0 * HW + share, h1 * HW)
-            issue_loads()
-            for g in range(2):
-                if MOM_IT[4 * g + 3] == it:
-                    for b in range(4):
-                        moment_out(nc.vector.tensor_copy if MO_E[4 * g + b] else nc.scalar.copy, g, b, bank[4 + b])
+        load_x(6)
+        load_num(3)
+        load_z(1)
+        x_round[1] = -1
+
+        for now in range(rounds):
+            if 1 <= now <= STEPS:
+                weigh(now - 1)
+            for pair in range(1, PAIRS):
+                if x_round[pair] == now - 1:
+                    quantize(x_codes[pair][:], x_plane[pair][:], flat(x_words[pair % 2][:]))
+            if now - 1 in side:
+                rows, codes, plane, words, c0, split, c1 = side[now - 1]
+                quantize_columns(codes, plane, words, c0, c1)
+            if now - 1 in weave_round:
+                swm_quantize(weave_round.index(now - 1))
+            for step in range(STEPS):
+                if turn_round[step] == now - 1:
+                    swc_quantize(step // 2, step % 2, step % 2 + 1)
+            if now in weave_round:
+                sw_weave(weave_round.index(now))
+            if now in side:
+                rows, codes, plane, words, c0, split, c1 = side[now]
+                interleave(nc.vector.tensor_copy, words, rows, c0, split)
+
+            if now < STEPS:
+                eta(now, 0)
+                eta(now, 1)
+                exponential(now, 0)
+                exponential(now, 1)
+            for pair in range(PAIRS):
+                if contrast_round[pair] == now:
+                    contrast(pair, now)
+            for step in range(STEPS):
+                if turn_round[step] == now:
+                    sw_turn(step, now)
+            for pair in range(2, PAIRS):
+                if x_round[pair] == now:
+                    x_transpose(pair, 0, now)
+                    x_transpose(pair, 1, now)
+                    x_evict(pair, 0)
+                    x_evict(pair, 1)
+            for g, j in moment_round:
+                if moment_round[g, j] == now:
+                    moment_pass(g, j)
+            if now in side:
+                interleave(nc.scalar.copy, words, rows, split, c1)
+
+            if now == x_round[2]:
+                load_x(7)
+                load_num(4)
+                load_v()
+                load_z(2)
+                load_z(3)
+            if now % 2 == 0 and NUM_TILES <= now // 2 - 1 + NUM_TILES <= last_unit:
+                load_num(now // 2 - 1 + NUM_TILES)
+            for g in range(HALVES):
+                if moment_round[g, GROUPS - 1] == now:
+                    moment_store(g)

@@ -156,8 +156,8 @@ def tile_inverse_propensity_weighted_sums_s8_kernel(tc, x, beta, num, z, v_words
 
         def x_evict(pair, slot):
             nc.scalar.copy(
-                out=x_words[pair % 2][:, slot, :].bitcast(F32).rearrange("p (c m u) -> p c m u", c=2, u=2),
-                in_=held["x", pair, slot][:].rearrange("p (c u m) -> p c m u", c=2, u=2),
+                out=x_words[pair % 2][:, slot, :].bitcast(F32).rearrange("p (c m i u) -> p c m u i", c=2, i=2, u=2),
+                in_=held["x", pair, slot][:].rearrange("p (c u m i) -> p c m u i", c=2, u=2, i=2),
             )
 
         def eta(step, slot):
@@ -207,8 +207,8 @@ def tile_inverse_propensity_weighted_sums_s8_kernel(tc, x, beta, num, z, v_words
                     packed = sw[unit % SW_TILES][:, u, 2 * h + slot, :].bitcast(F32)
                     nc.tensor.transpose(acc[:, col : col + P], packed, ident[:])
             nc.scalar.copy(
-                out=flat(swc_words[unit % 2][:, HW * h : HW * (h + 1), :]).bitcast(F32).rearrange("p (a m u) -> p a m u", a=2, u=2),
-                in_=acc[:].rearrange("p (a u m) -> p a m u", a=2, u=2),
+                out=flat(swc_words[unit % 2][:, HW * h : HW * (h + 1), :]).bitcast(F32).rearrange("p (a m i u) -> p a m u i", a=2, i=2, u=2),
+                in_=acc[:].rearrange("p (a u m i) -> p a m u i", a=2, u=2, i=2),
             )
 
         def swc_quantize(unit, h0, h1):

from contextlib import ExitStack

import concourse.mybir as mybir
from concourse.masks import make_identity

M, K, N, R, Z_COLS = 2048, 1024, 1024, 512, 512
FLOPS = 2 * M * K * N + 2 * M * N * R + 2 * Z_COLS * M * N

F32 = mybir.dt.float32
BF16 = mybir.dt.bfloat16
U32 = mybir.dt.uint32
I32 = mybir.dt.int32
U8 = mybir.dt.uint8
FP8X4 = mybir.dt.float8_e4m3fn_x4
FP4X4 = mybir.dt.float4_e2m1fn_x4
ALU = mybir.AluOpType
ACT = mybir.ActivationFunctionType

P = 128
W = 512
HW = W // 2
GROUPS, HALVES = M // W, N // W
PAIRS = 2 * GROUPS
STEPS = 2 * GROUPS * HALVES

UNITS = [(0, 0), (1, 0), (0, 1), (2, 0), (3, 0), (1, 1), (2, 1), (3, 1)]

X_LEAD = 3
TURN_LAG = 2
USE_LAG = 2
BETA_ROUND = 1
Z_ROUND = 4

SHARE_EARLY, SHARE_LATE = 0.75, 0.25

X_TILES, NUM_TILES, SW_TILES, CONTRAST_TILES = 5, 5, 3, 3


def tile_inverse_propensity_weighted_sums_s8_kernel(tc, x, beta, num, z, v_words, v_scales, out_0, out_1):
    nc = tc.nc
    with ExitStack() as ctx:
        sb = ctx.enter_context(tc.tile_pool(name="sb", bufs=1))
        ps = ctx.enter_context(tc.psum_pool(name="ps", bufs=1))
        ctx.enter_context(tc.manual_schedule())

        def tiles(name, count, shape, dtype):
            return [sb.tile(shape, dtype, name="%s%d" % (name, i), align_bytes=64) for i in range(count)]

        def flat(view):
            return view.rearrange("p a b -> p (a b)")

        unit_of = {key: unit for unit, key in enumerate(UNITS)}
        last_unit = len(UNITS) - 1
        x_round = {}
        for pair in range(2, PAIRS):
            first_step = 2 * unit_of[pair // 2, 0] + pair % 2
            x_round[pair] = max(first_step - X_LEAD, pair - 2)
        turn_round = [s + TURN_LAG - (1 if s // 2 == last_unit else 0) for s in range(STEPS)]
        weave_round = [2 * unit + (2 if unit == last_unit else 3) for unit in range(len(UNITS))]
        z_round = [Z_ROUND + job for job in range(2 * GROUPS)]
        moment_round = {}
        previous = 0
        for g in range(HALVES):
            for j in range(GROUPS):
                ready = max(weave_round[unit_of[j, g]], z_round[2 * j + 1]) + USE_LAG
                previous = max(ready, previous + 1)
                moment_round[g, j] = previous
        contrast_round = [turn_round[2 * unit_of[pair // 2, 1] + pair % 2] + USE_LAG for pair in range(PAIRS)]
        contrast_round[-1] = previous + 1
        rounds = contrast_round[-1] + 1

        bank = [ps.tile([P, W], F32, name="bank%d" % i) for i in range(8)]
        moment_bank = bank[4:]
        held = {}
        cursor = [0]

        def take_bank(key, now):
            count = 8 if now < moment_round[0, 0] else 4
            held[key] = bank[cursor[0] % count]
            cursor[0] = (cursor[0] + 1) % count
            return held[key]

        ident = sb.tile([P, P], F32, name="ident", align_bytes=64)
        warm = sb.tile([P, 8], F32, name="warm", align_bytes=64)
        x_first = tiles("x_first", 2, [P, K], BF16)
        x_raw = tiles("x_raw", X_TILES, [P, 2, K], BF16)
        beta_raw = tiles("beta_raw", 4, [P, 4, W], BF16)
        z_raw = tiles("z_raw", 2, [P, 4, W], BF16) + beta_raw[:2]
        num_raw = tiles("num_raw", NUM_TILES, [P, 4, W], BF16)
        v_codes = sb.tile([P, HALVES, 2 * R], U8, name="v_codes", align_bytes=64)
        v_plane = sb.tile([P, HALVES, R], U8, name="v_plane", align_bytes=64)

        x_codes, x_plane = tiles("x_codes", PAIRS, [P, W], U32), tiles("x_plane", PAIRS, [P, W], U8)
        beta_codes, beta_plane = tiles("beta_codes", 4, [P, W], U32), tiles("beta_plane", 4, [P, W], U8)
        z_codes, z_plane = tiles("z_codes", GROUPS, [P, W], U32), tiles("z_plane", GROUPS, [P, W], U8)
        swm_codes, swm_plane = tiles("swm_codes", 8, [P, W], U32), tiles("swm_plane", 8, [P, W], U8)
        swc_codes, swc_plane = tiles("swc_codes", 8, [P, W], U32), tiles("swc_plane", 8, [P, W], U8)

        x_words = tiles("x_words", 2, [P, 2, 2 * W], BF16)
        side_words = tiles("side_words", 2, [P, W, 4], BF16)
        swm_words = tiles("swm_words", 2, [P, W, 4], BF16)
        exp_eta = tiles("exp_eta", 2, [P, 2, 4, HW], F32)
        sw = tiles("sw", SW_TILES, [P, 2, 4, HW], BF16)
        swc_words = tiles("swc_words", 2, [P, W, 4], BF16)
        contrast_out = tiles("contrast_out", CONTRAST_TILES, [P, 2, R], F32)
        moment_out = tiles("moment_out", 4, [P, W], F32)

        x_v = x.rearrange("(j p t) k -> j p t k", p=P, t=4)
        num_v = num.rearrange("(j p t) n -> j p t n", p=P, t=4)
        z_v = z.rearrange("(j p t) c -> j p t c", p=P, t=4)
        beta_v = beta.rearrange("(c p t) n -> c p t n", p=P, t=4)
        contrast_v = out_0.rearrange("(j p t) r -> j p t r", p=P, t=4)

        def load_x(pair):
            j, h = divmod(pair, 2)
            nc.sync.dma_start(out=x_raw[(pair - 1) % X_TILES][:], in_=x_v[j][:, 2 * h : 2 * h + 2, :])

        def load_beta(g, c):
            nc.sync.dma_start(out=beta_raw[2 * g + c][:], in_=beta_v[c][:, :, g * W : (g + 1) * W])

        def load_num(unit):
            j, g = UNITS[unit]
            nc.sync.dma_start(out=num_raw[unit % NUM_TILES][:], in_=num_v[j][:, :, g * W : (g + 1) * W])

        def load_z(j):
            nc.sync.dma_start(out=z_raw[j][:], in_=z_v[j])

        def load_v():
            nc.sync.dma_start(out=v_codes[:].bitcast(I32), in_=v_words.rearrange("g p b -> p g b").bitcast(I32))
            for quad in range(4):
                nc.sync.dma_start(
                    out=v_plane[32 * quad : 32 * quad + 4, :, :].bitcast(I32),
                    in_=v_scales[:, 4 * quad : 4 * quad + 4, :].rearrange("g r n -> r g n").bitcast(I32),
                )

        def interleave(copy, words, rows, c0, c1):
            copy(
                out=words[:, c0:c1, :].rearrange("p (c i) t -> p c t i", i=4),
                in_=rows[:, :, c0:c1].rearrange("p t (c i) -> p c t i", i=4),
            )

        def quantize(codes, plane, values):
            nc.vector.quantize_mx(out=codes.bitcast(FP8X4), scales=plane, in_=values)

        def quantize_columns(codes, plane, words, c0, c1):
            quantize(codes[:, c0:c1], plane[:, c0:c1], flat(words[:, c0:c1, :]))

        def x_transpose(pair, slot, now):
            rows = x_first[slot][:] if pair == 0 else x_raw[(pair - 1) % X_TILES][:, slot, :]
            packed = rows.bitcast(F32)
            acc = take_bank(("x", pair, slot), now)
            for c in range(2):
                for u in range(2):
                    col = (2 * c + u) * P
                    nc.tensor.transpose(acc[:, col : col + P], packed[:, HW * c + u : HW * (c + 1) : 2], ident[:])

        def x_evict(pair, slot):
            nc.scalar.copy(
                out=x_words[pair % 2][:, slot, :].bitcast(F32).rearrange("p (c m i u) -> p c m u i", c=2, i=2, u=2),
                in_=held["x", pair, slot][:].rearrange("p (c u m i) -> p c m u i", c=2, u=2, i=2),
            )

        def eta(step, slot):
            j, g = UNITS[step // 2]
            pair = 2 * j + step % 2
            acc = take_bank(("eta", step, slot), step)
            for c in range(2):
                cols = slice((2 * slot + c) * P, (2 * slot + c + 1) * P)
                nc.tensor.matmul_mx(
                    out=acc[:],
                    lhsT=x_codes[pair][:, cols].bitcast(FP8X4),
                    lhsT_scale=x_plane[pair][:, cols],
                    rhs=beta_codes[2 * g + c][:].bitcast(FP8X4),
                    rhs_scale=beta_plane[2 * g + c][:],
                    start=(c == 0),
                    stop=(c == 1),
                )

        def exponential(step, slot):
            unit, h = divmod(step, 2)
            nc.scalar.activation(
                out=exp_eta[unit % 2][:, :, 2 * h + slot, :].rearrange("p u (q e) -> p u q e", e=2),
                in_=held["eta", step, slot][:].rearrange("p (q u e) -> p u q e", u=2, e=2),
                func=ACT.Exp,
            )

        def weigh(step):
            unit, h = divmod(step, 2)
            slots = slice(2 * h, 2 * h + 2)
            numerators = flat(num_raw[unit % NUM_TILES][:, slots, :]).rearrange("p (a u e) -> p u a e", u=2, e=2)
            for u in range(2):
                nc.vector.scalar_tensor_tensor(
                    out=flat(sw[unit % SW_TILES][:, u, slots, :]).rearrange("p (a e) -> p a e", e=2),
                    in0=flat(exp_eta[unit % 2][:, u, slots, :]).rearrange("p (a e) -> p a e", e=2),
                    scalar=1.0,
                    in1=numerators[:, u, :, :],
                    op0=ALU.add,
                    op1=ALU.mult,
                )

        def sw_turn(step, now):
            unit, h = divmod(step, 2)
            acc = take_bank(("sw", step), now)
            for slot in range(2):
                for u in range(2):
                    col = (2 * slot + u) * P
                    packed = sw[unit % SW_TILES][:, u, 2 * h + slot, :].bitcast(F32)
                    nc.tensor.transpose(acc[:, col : col + P], packed, ident[:])
            nc.scalar.copy(
                out=flat(swc_words[unit % 2][:, HW * h : HW * (h + 1), :]).bitcast(F32).rearrange("p (a m i u) -> p a m u i", a=2, i=2, u=2),
                in_=acc[:].rearrange("p (a u m i) -> p a m u i", a=2, u=2, i=2),
            )

        def swc_quantize(unit, h0, h1):
            j, g = UNITS[unit]
            quantize_columns(swc_codes[4 * g + j], swc_plane[4 * g + j], swc_words[unit % 2], HW * h0, HW * h1)

        def sw_weave(unit):
            nc.vector.tensor_copy(
                out=swm_words[unit % 2][:].rearrange("p (u c i) t -> p u c t i", u=2, i=4),
                in_=sw[unit % SW_TILES][:].rearrange("p u t (c i) -> p u c t i", i=4),
            )

        def swm_quantize(unit):
            j, g = UNITS[unit]
            quantize_columns(swm_codes[4 * g + j], swm_plane[4 * g + j], swm_words[unit % 2], 0, W)

        def contrast(pair, now):
            j, h = divmod(pair, 2)
            result = contrast_out[pair % CONTRAST_TILES]
            for slot in range(2):
                acc = take_bank(("contrast", pair, slot), now)
                cols = slice((2 * h + slot) * P, (2 * h + slot + 1) * P)
                for g in range(HALVES):
                    nc.tensor.matmul_mx(
                        out=acc[:],
                        lhsT=swc_codes[4 * g + j][:, cols].bitcast(FP8X4),
                        lhsT_scale=swc_plane[4 * g + j][:, cols],
                        rhs=v_codes[:, g, :].bitcast(FP4X4),
                        rhs_scale=v_plane[:, g, :],
                        start=(g == 0),
                        stop=(g == HALVES - 1),
                    )
                copy = nc.vector.tensor_copy if (pair, slot) == (PAIRS - 1, 1) else nc.scalar.copy
                copy(out=result[:, slot, :], in_=acc[:])
            nc.sync.dma_start(out=contrast_v[j][:, 2 * h : 2 * h + 2, :], in_=result[:])

        def moment_pass(g, j):
            for b in range(4):
                cols = slice(b * P, (b + 1) * P)
                nc.tensor.matmul_mx(
                    out=moment_bank[b][:],
                    lhsT=z_codes[j][:, cols].bitcast(FP8X4),
                    lhsT_scale=z_plane[j][:, cols],
                    rhs=swm_codes[4 * g + j][:].bitcast(FP8X4),
                    rhs_scale=swm_plane[4 * g + j][:],
                    start=(j == 0),
                    stop=(j == GROUPS - 1),
                )

        def moment_store(g):
            for b in range(4):
                copy = nc.vector.tensor_copy if b % 2 else nc.scalar.copy
                copy(
                    out=moment_out[b][:].rearrange("p (q u e) -> p q u e", u=2, e=2),
                    in_=moment_bank[b][:].rearrange("p (u q e) -> p q u e", u=2, e=2),
                )
                nc.sync.dma_start(out=out_1[b * P : (b + 1) * P, g * W : (g + 1) * W], in_=moment_out[b][:])

        side = {}
        for c in range(2):
            job = (beta_raw[2 + c], beta_codes[2 + c], beta_plane[2 + c], side_words[c], 0, int(SHARE_EARLY * W), W)
            side[BETA_ROUND + c] = job
        for job_index in range(2 * GROUPS):
            j, part = divmod(job_index, 2)
            split = HW * part + int((SHARE_EARLY if j < 2 else SHARE_LATE) * HW)
            side[z_round[job_index]] = (z_raw[j], z_codes[j], z_plane[j], side_words[j % 2], HW * part, split, HW * (part + 1))

        nc.sync.dma_start(out=x_first[0][:], in_=x_v[0][:, 0, :])
        load_beta(0, 0)
        load_beta(0, 1)
        nc.sync.dma_start(out=x_first[1][:], in_=x_v[0][:, 1, :])
        make_identity(nc, ident[:])
        nc.vector.memset(warm[:], 0.0)
        nc.scalar.activation(out=warm[:, 4:5], in_=warm[:, 0:1], func=ACT.Exp)
        nc.vector.memset(flat(v_plane[:]).bitcast(I32), 0)
        load_x(1)
        load_num(0)
        load_x(2)
        load_beta(1, 0)
        load_x(3)
        load_num(1)
        load_beta(1, 1)
        load_x(4)
        load_x(5)
        load_num(2)
        load_z(0)

        split = int(SHARE_EARLY * W)
        x_transpose(0, 0, -1)
        x_evict(0, 0)
        interleave(nc.vector.tensor_copy, side_words[0], beta_raw[0], 0, split)
        interleave(nc.scalar.copy, side_words[0], beta_raw[0], split, W)
        quantize(x_codes[0][:, :HW], x_plane[0][:, :HW], x_words[0][:, 0, :])
        quantize_columns(beta_codes[0], beta_plane[0], side_words[0], 0, W)
        interleave(nc.vector.tensor_copy, side_words[1], beta_raw[1], 0, split)
        interleave(nc.scalar.copy, side_words[1], beta_raw[1], split, W)
        x_transpose(0, 1, -1)
        x_evict(0, 1)
        x_transpose(1, 0, -1)
        x_transpose(1, 1, -1)
        quantize_columns(beta_codes[1], beta_plane[1], side_words[1], 0, W)
        quantize(x_codes[0][:, HW:], x_plane[0][:, HW:], x_words[0][:, 1, :])
        x_evict(1, 0)
        x_evict(1, 1)
        load_x(6)
        load_num(3)
        load_z(1)
        x_round[1] = -1

        for now in range(rounds):
            if 1 <= now <= STEPS:
                weigh(now - 1)
            for pair in range(1, PAIRS):
                if x_round[pair] == now - 1:
                    quantize(x_codes[pair][:], x_plane[pair][:], flat(x_words[pair % 2][:]))
            if now - 1 in side:
                rows, codes, plane, words, c0, split, c1 = side[now - 1]
                quantize_columns(codes, plane, words, c0, c1)
            if now - 1 in weave_round:
                swm_quantize(weave_round.index(now - 1))
            for step in range(STEPS):
                if turn_round[step] == now - 1:
                    swc_quantize(step // 2, step % 2, step % 2 + 1)
            if now in weave_round:
                sw_weave(weave_round.index(now))
            if now in side:
                rows, codes, plane, words, c0, split, c1 = side[now]
                interleave(nc.vector.tensor_copy, words, rows, c0, split)

            if now < STEPS:
                eta(now, 0)
                eta(now, 1)
                exponential(now, 0)
                exponential(now, 1)
            for pair in range(PAIRS):
                if contrast_round[pair] == now:
                    contrast(pair, now)
            for step in range(STEPS):
                if turn_round[step] == now:
                    sw_turn(step, now)
            for pair in range(2, PAIRS):
                if x_round[pair] == now:
                    x_transpose(pair, 0, now)
                    x_transpose(pair, 1, now)
                    x_evict(pair, 0)
                    x_evict(pair, 1)
            for g, j in moment_round:
                if moment_round[g, j] == now:
                    moment_pass(g, j)
            if now in side:
                interleave(nc.scalar.copy, words, rows, split, c1)

            if now == x_round[2]:
                load_x(7)
                load_num(4)
                load_v()
                load_z(2)
                load_z(3)
            if now % 2 == 0 and NUM_TILES <= now // 2 - 1 + NUM_TILES <= last_unit:
                load_num(now // 2 - 1 + NUM_TILES)
            for g in range(HALVES):
                if moment_round[g, GROUPS - 1] == now:
                    moment_store(g)
